import numpy as np
import ml_dtypes


def mxq(x, axis, fmt="e4m3"):
    dtype, down = {"e4m3": (ml_dtypes.float8_e4m3fn, 7), "e5m2": (ml_dtypes.float8_e5m2, 14)}[fmt]
    v = np.moveaxis(np.asarray(x, np.float32).astype(ml_dtypes.bfloat16).astype(np.float64), axis, -1)
    blocks = v.reshape(v.shape[:-1] + (-1, 32))
    amax = np.abs(blocks).max(-1, keepdims=True)
    byte = np.maximum(np.where(amax > 0, np.frexp(amax)[1] - 1 + 127, 0) - down, 1)
    scale = np.exp2(byte - 127.0)
    codes = (blocks / scale).astype(np.float32).astype(dtype).astype(np.float64)
    return np.moveaxis((codes * scale).reshape(v.shape), -1, axis)


WIDE = False


def mx_kscale(k):
    if not WIDE:
        return np.ones(k)
    levels = np.array([10, -10, 5, -5, 0])
    if k % 512:
        return np.exp2(np.random.permutation(np.resize(levels, k // 32))).repeat(32)
    a = np.empty((k // 512, 16))
    for p in range(k // 512):
        a[p, :8] = np.random.permutation(np.resize(levels, 8))
        for g in range(8):
            far = levels[np.abs(levels - a[p, g]) >= 10]
            a[p, g + 8] = far[np.random.randint(len(far))]
    return np.exp2(a.ravel()).repeat(32)


def f64(x):
    return np.asarray(x).astype(np.float64)


def striped(idx):
    return np.tile(idx.reshape(-1, 16).T, (8, 1)).astype(np.uint16)


def unstriped(offs):
    return offs[:16].T.reshape(-1).astype(np.int64)


E2M1 = np.array([0.0, 0.5, 1.0, 1.5, 2.0, 3.0, 4.0, 6.0, -0.0, -0.5, -1.0, -1.5, -2.0, -3.0, -4.0, -6.0])


def pack_weight(w, fmt):
    k, n = w.shape
    w = f64(np.asarray(w, np.float32).astype(ml_dtypes.bfloat16)).reshape(k // 32, 32, n)
    amax = np.abs(w).max(1)
    if fmt == "e4m3":
        byte = np.frexp(amax)[1] - 1 + 127 - 7
    else:
        mant, ex = np.frexp(amax / 6.0)
        byte = np.where(mant > 0.5, ex, ex - 1) + 127
    byte = np.clip(np.where(amax > 0, byte, 1), 1, 254)
    scaled = (w * np.exp2(127.0 - byte)[:, None, :]).reshape(k, n).astype(np.float32)
    by_word = np.ascontiguousarray(scaled.reshape(k // 512, 128, 4, n).transpose(0, 1, 3, 2))
    if fmt == "e4m3":
        words = by_word.astype(ml_dtypes.float8_e4m3fn).view(np.uint8)
    else:
        c = by_word.astype(ml_dtypes.float4_e2m1fn).view(np.uint8) & 0xF
        words = (c[..., 0::2] | (c[..., 1::2] << 4)).reshape(k // 512, 128, 2 * n)
    return np.ascontiguousarray(words), np.ascontiguousarray(byte.astype(np.uint8).reshape(k // 512, 16, n))


def unpack_weight(words, scales, fmt):
    g, _, n = scales.shape
    words = np.ascontiguousarray(words).reshape(g, 128, n, -1)
    if fmt == "e4m3":
        vals = words.view(ml_dtypes.float8_e4m3fn).astype(np.float64)
    else:
        nib = np.empty((g, 128, n, 4), np.uint8)
        nib[..., 0::2] = words & 0xF
        nib[..., 1::2] = words >> 4
        vals = E2M1[nib]
    vals = vals * np.repeat(np.exp2(scales.astype(np.float64) - 127.0), 8, axis=1)[..., None]
    return vals.transpose(0, 1, 3, 2).reshape(g * 512, n)


def gelu(v):
    return 0.5 * v * (1.0 + np.tanh(np.sqrt(2.0 / np.pi) * (v + 0.044715 * v**3)))


K, T, S, S2 = 1024, 4096, 1024, 512

def setup_inputs():
    n = np.random.standard_normal
    s = mx_kscale(K)[:, None]
    d = {}
    d["tab_words"], d["tab_scales"] = pack_weight(n((K, T)) * s, "e4m3")
    d["offs"] = striped(np.random.permutation(T)[:S])
    d["offs2"] = striped(np.random.permutation(T)[:S2])
    d["w1"] = (1.4 * n((K, K)) / s / s.T / K).astype(np.float32)
    d["w4_words"], d["w4_scales"] = pack_weight(n((K, S2)) / s / K**0.5, "e2m1")
    d["sharp"] = (0.8 * np.exp(0.4 * n(S2))).astype(np.float32)
    return d

def reference(tab_words, tab_scales, offs, offs2, w1, w4_words, w4_scales, sharp):
    TW = unpack_weight(tab_words, tab_scales, "e4m3")
    v = TW[:, unstriped(offs)]
    v2 = TW[:, unstriped(offs2)]
    w4 = unpack_weight(w4_words, w4_scales, "e2m1")
    h = np.maximum(mxq(f64(w1), 0, "e4m3").T @ v, 0.0)
    e = v2.T @ mxq(h, 0, "e4m3")
    f = w4.T @ v
    gap = np.abs(e - f)
    return np.exp(-(f64(sharp)[:, None] * gap))

@@ -1,0 +1,269 @@
+from contextlib import ExitStack
+
+import concourse.mybir as mybir
+
+K, T, S, S2 = 1024, 4096, 1024, 512
+FLOPS = 2 * K * K * S + 2 * 2 * K * S2 * S
+
+F32 = mybir.dt.float32
+BF16 = mybir.dt.bfloat16
+I32 = mybir.dt.int32
+U32 = mybir.dt.uint32
+U16 = mybir.dt.uint16
+U8 = mybir.dt.uint8
+FP8X4 = mybir.dt.float8_e4m3fn_x4
+FP4X4 = mybir.dt.float4_e2m1fn_x4
+ALU = mybir.AluOpType
+ACT = mybir.ActivationFunctionType
+
+P = 128
+PACK = 4
+KP = P * PACK
+PASSES = K // KP
+HALF = 512
+JT = 128
+PER_COL = 16
+
+LOAD_PIECES = {
+    (0, 0): [(0, 512)],
+    (1, 0): [(0, 512)],
+    (0, 1): [(0, 512)],
+    (1, 1): [(0, 512)],
+}
+CASTS = {
+    (0, 0): [(0, 512, "s")],
+    (1, 0): [(0, 512, "s")],
+    (0, 1): [(0, 512, "s")],
+    (1, 1): [(0, 512, "s")],
+}
+SCALAR_EVAC = {(0, 0), (0, 2), (1, 0), (1, 1), (1, 2), (1, 3)}
+VECTOR_ABS = {(0, 1), (1, 1), (3, 1)}
+
+
+def tile_list_logo_conflict_likeness_kernel(
+    tc, tab_words, tab_scales, offs, offs2, w1, w4_words, w4_scales, sharp, out
+):
+    nc = tc.nc
+    with ExitStack() as ctx:
+        lists = ctx.enter_context(tc.tile_pool(name="lists", bufs=1))
+        keep = ctx.enter_context(tc.tile_pool(name="keep", bufs=1))
+        ring = ctx.enter_context(tc.tile_pool(name="ring", bufs=4))
+        psum = ctx.enter_context(tc.psum_pool(name="psum", bufs=1))
+
+        idx = lists.tile([P, S // PER_COL], U16, name="idx")
+        idx2 = lists.tile([P, S2 // PER_COL], U16, name="idx2")
+        tab = [keep.tile([P, T], I32, name="tab%d" % a, align_bytes=64) for a in range(PASSES)]
+        tab_sc = keep.tile([P, T], U8, name="tab_sc", align_bytes=64)
+        w4 = keep.tile([P, PASSES, 2 * S2], U8, name="w4", align_bytes=64)
+        w4_sc = keep.tile([P, PASSES, S2], U8, name="w4_sc", align_bytes=64)
+        v_sc = keep.tile([P, S], U8, name="v_sc", align_bytes=64)
+        v_sc1 = keep.tile([P, S], U8, name="v_sc1", align_bytes=64)
+        v2_sc = keep.tile([P, S2], U8, name="v2_sc", align_bytes=64)
+        v = [[keep.tile([P, HALF], U32, name="v%d_%d" % (a, h), align_bytes=64) for h in range(2)] for a in range(PASSES)]
+        v2 = [keep.tile([P, S2], U32, name="v2_%d" % a, align_bytes=64) for a in range(PASSES)]
+        sharp_sb = keep.tile([P, S2 // P], F32, name="sharp_sb")
+        neg_sharp = keep.tile([P, S2 // P], F32, name="neg_sharp")
+        warm_in = keep.tile([P, 1], F32, name="warm_in")
+        warm_out = keep.tile([P, 1], F32, name="warm_out")
+
+        w_raw, w_bf, w_q, w_sc, h_bf, h_q, h_sc = {}, {}, {}, {}, {}, {}, {}
+        for a in range(PASSES):
+            for b in range(PASSES):
+                w_raw[a, b] = [
+                    keep.tile([P, PACK, c1 - c0], F32, name="wraw%d%d_%d" % (a, b, c0))
+                    for c0, c1 in LOAD_PIECES[a, b]
+                ]
+                w_bf[a, b] = keep.tile([P, PACK, P, PACK], BF16, name="wbf%d%d" % (a, b), align_bytes=64)
+                w_q[a, b] = keep.tile([P, KP], U32, name="wq%d%d" % (a, b), align_bytes=64)
+                w_sc[a, b] = keep.tile([P, KP], U8, name="wsc%d%d" % (a, b), align_bytes=64)
+                h_bf[a, b] = keep.tile([P, HALF * PACK], BF16, name="hbf%d%d" % (a, b), align_bytes=64)
+                h_q[a, b] = keep.tile([P, HALF], U32, name="hq%d%d" % (a, b), align_bytes=64)
+                h_sc[a, b] = keep.tile([P, HALF], U8, name="hsc%d%d" % (a, b), align_bytes=64)
+
+        def bank(n):
+            return psum.tile([P, HALF], F32, name="bank%d" % n, tag="bank%d" % n)
+
+        def load_tab(a):
+            nc.sync.dma_start(tab[a][:], tab_words[a].rearrange("p n i -> p (n i)").bitcast(I32))
+
+        def load_w(a, b):
+            rows = w1[a * KP : (a + 1) * KP, b * KP : (b + 1) * KP].rearrange("(p i) c -> p i c", i=PACK)
+            for raw, (c0, c1) in zip(w_raw[a, b], LOAD_PIECES[a, b]):
+                nc.sync.dma_start(raw[:], rows[:, :, c0:c1])
+
+        def cast_w(a, b):
+            for c0, c1, engine in CASTS[a, b]:
+                for raw, (p0, p1) in zip(w_raw[a, b], LOAD_PIECES[a, b]):
+                    if p0 <= c0 and c1 <= p1:
+                        src = raw[:, :, c0 - p0 : c1 - p0].rearrange("p i (m t) -> p m i t", t=PACK)
+                        dst = w_bf[a, b][:, :, c0 // PACK : c1 // PACK, :].rearrange("p t m i -> p m i t")
+                        if engine == "s":
+                            nc.scalar.copy(dst, src)
+                        else:
+                            nc.vector.tensor_copy(dst, src)
+
+        def quantize_w(a, b):
+            nc.vector.quantize_mx(
+                out=w_q[a, b][:].bitcast(FP8X4),
+                scales=w_sc[a, b][:],
+                in_=w_bf[a, b][:].rearrange("p t m i -> p (t m i)"),
+            )
+
+        def gather_v(a, h):
+            cols = slice(h * HALF // PER_COL, (h + 1) * HALF // PER_COL)
+            nc.vector.tensor_copy(v[a][h][:], tab[a][:].bitcast(U32).indirect(idx[:, cols]))
+
+        def gather_v2(a):
+            nc.vector.tensor_copy(v2[a][:], tab[a][:].bitcast(U32).indirect(idx2[:]))
+
+        def first_product(acc, a, b, jt):
+            h, j0 = divmod(jt * JT, HALF)
+            for t in range(PACK):
+                nc.tensor.matmul_mx(
+                    out=acc[:, t * JT : (t + 1) * JT],
+                    lhsT=w_q[a, b][:, t * P : (t + 1) * P].bitcast(FP8X4),
+                    lhsT_scale=w_sc[a, b][:, t * P : (t + 1) * P],
+                    rhs=v[a][h][:, j0 : j0 + JT].bitcast(FP8X4),
+                    rhs_scale=v_sc[4 * a : P, jt * JT : (jt + 1) * JT],
+                    start=(a == 0 and t == 0),
+                    stop=(a == PASSES - 1 and t == PACK - 1),
+                )
+
+        def rectify(acc, b, jt):
+            h, j0 = divmod(jt * JT, HALF)
+            src = acc[:].rearrange("p (t j) -> p j t", t=PACK)
+            flat = h_bf[b, h][:, j0 * PACK : (j0 + JT) * PACK]
+            if (b, jt) in SCALAR_EVAC:
+                pos = ring.tile([P, JT * PACK], BF16, name="pos")
+                nc.scalar.activation(pos[:].rearrange("p (j t) -> p j t", t=PACK), src, ACT.Relu)
+                nc.vector.tensor_scalar(flat, pos[:], -1.0, None, ALU.mult)
+            else:
+                nc.vector.tensor_scalar(flat.rearrange("p (j t) -> p j t", t=PACK), src, -1.0, 0.0, ALU.mult, ALU.min)
+
+        def quantize_h(b, h):
+            nc.vector.quantize_mx(out=h_q[b, h][:].bitcast(FP8X4), scales=h_sc[b, h][:], in_=h_bf[b, h][:])
+
+        def skip_product(acc, a, mt, h):
+            plane = v_sc if a == 0 else v_sc1
+            nc.tensor.matmul_mx(
+                out=acc[:],
+                lhsT=w4[:, a, 2 * mt * P : 2 * (mt + 1) * P].bitcast(FP4X4),
+                lhsT_scale=w4_sc[:, a, mt * P : (mt + 1) * P],
+                rhs=v[a][h][:].bitcast(FP8X4),
+                rhs_scale=plane[:, h * HALF : (h + 1) * HALF],
+                start=(a == 0),
+                stop=False,
+            )
+
+        def match_product(acc, b, mt, h):
+            nc.tensor.matmul_mx(
+                out=acc[:],
+                lhsT=v2[b][:, mt * P : (mt + 1) * P].bitcast(FP8X4),
+                lhsT_scale=v2_sc[4 * b : P, mt * P : (mt + 1) * P],
+                rhs=h_q[b, h][:].bitcast(FP8X4),
+                rhs_scale=h_sc[b, h][:],
+                start=False,
+                stop=(b == PASSES - 1),
+            )
+
+        def likeness(acc, mt, h):
+            gap = ring.tile([P, HALF], F32, name="gap")
+            like = ring.tile([P, HALF], F32, name="like")
+            if (mt, h) in VECTOR_ABS:
+                diff = ring.tile([P, HALF], F32, name="diff")
+                nc.vector.tensor_copy(diff[:], acc[:])
+                nc.vector.scalar_tensor_tensor(gap[:], diff[:], -1.0, diff[:], ALU.mult, ALU.max)
+            else:
+                nc.scalar.activation(gap[:], acc[:], ACT.Abs)
+            nc.scalar.activation(like[:], gap[:], ACT.Exp, scale=neg_sharp[:, mt : mt + 1])
+            nc.sync.dma_start(out[mt * P : (mt + 1) * P, h * HALF : (h + 1) * HALF], like[:])
+
+        nc.vector.memset(tab_sc[:].bitcast(I32), 0)
+        nc.gpsimd.memset(w4_sc[:].rearrange("p a c -> p (a c)").bitcast(I32), 0)
+        nc.gpsimd.memset(v_sc1[:].bitcast(I32), 0)
+        nc.vector.memset(warm_in[:], 0.0)
+        nc.scalar.activation(warm_out[:], warm_in[:], ACT.Exp)
+
+        nc.sync.dma_start(idx[:], offs)
+        load_w(0, 0)
+        nc.sync.dma_start(idx2[:], offs2)
+        load_tab(0)
+        for q in range(4):
+            nc.gpsimd.dma_start(
+                tab_sc[32 * q : 32 * q + 4 * PASSES, :].bitcast(I32),
+                tab_scales[:, 4 * q : 4 * q + 4, :].bitcast(I32),
+            )
+        for q in range(4):
+            nc.gpsimd.dma_start(
+                w4_sc[32 * q : 32 * q + 4, :, :].bitcast(I32),
+                w4_scales[:, 4 * q : 4 * q + 4, :].rearrange("a r c -> r a c").bitcast(I32),
+            )
+        load_w(1, 0)
+        load_tab(1)
+        nc.sync.dma_start(w4[:].bitcast(I32), w4_words.rearrange("a p c -> p a c").bitcast(I32))
+        load_w(0, 1)
+        load_w(1, 1)
+        with nc.allow_non_contiguous_dma(reason="one factor for each partition"):
+            nc.sync.dma_start(sharp_sb[:], sharp.rearrange("(c p) -> p c", p=P))
+        nc.gpsimd.tensor_scalar(neg_sharp[:], sharp_sb[:], -1.0, 0.0, ALU.mult, ALU.add)
+
+        nc.vector.tensor_copy(v_sc[:], tab_sc[:].indirect(idx[:]))
+        nc.gpsimd.dma_start(v_sc1[0:100, :].bitcast(I32), v_sc[4:104, :].bitcast(I32))
+        cast_w(0, 0)
+        quantize_w(0, 0)
+        gather_v(0, 0)
+        gather_v(0, 1)
+        nc.vector.tensor_copy(v2_sc[:], tab_sc[:].indirect(idx2[:]))
+        gather_v2(0)
+
+        tiles = S // JT
+        acc = [bank(n) for n in range(tiles)]
+        for jt in range(tiles):
+            first_product(acc[jt], 0, 0, jt)
+
+        cast_w(1, 0)
+        quantize_w(1, 0)
+        gather_v(1, 0)
+        gather_v(1, 1)
+
+        for jt in range(tiles):
+            first_product(acc[jt], 1, 0, jt)
+            rectify(acc[jt], 0, jt)
+
+        cast_w(0, 1)
+        quantize_w(0, 1)
+        quantize_h(0, 0)
+        res = [bank(mt) for mt in range(4)]
+        for a in range(PASSES):
+            for mt in range(4):
+                skip_product(res[mt], a, mt, 0)
+        acc = [bank(4 + n) for n in range(4)]
+        for jt in range(4):
+            first_product(acc[jt], 0, 1, jt)
+        cast_w(1, 1)
+        quantize_w(1, 1)
+        gather_v2(1)
+        quantize_h(0, 1)
+        for mt in range(4):
+            match_product(res[mt], 0, mt, 0)
+        for jt in range(4):
+            first_product(acc[jt], 1, 1, jt)
+            rectify(acc[jt], 1, jt)
+        quantize_h(1, 0)
+        for jt in range(4, 8):
+            acc = bank(jt)
+            for a in range(PASSES):
+                first_product(acc, a, 1, jt)
+            rectify(acc, 1, jt)
+            if jt == 5:
+                for mt in range(4):
+                    match_product(res[mt], 1, mt, 0)
+                    likeness(res[mt], mt, 0)
+        quantize_h(1, 1)
+        for mt in range(4):
+            res1 = bank(4 + mt)
+            for a in range(PASSES):
+                skip_product(res1, a, mt, 1)
+            for b in range(PASSES):
+                match_product(res1, b, mt, 1)
+            likeness(res1, mt, 1)

@@ -26,17 +26,17 @@ PER_COL = 16
 
 LOAD_PIECES = {
     (0, 0): [(0, 512)],
-    (1, 0): [(0, 512)],
+    (1, 0): [(0, 256), (256, 512)],
     (0, 1): [(0, 512)],
     (1, 1): [(0, 512)],
 }
 CASTS = {
     (0, 0): [(0, 512, "s")],
-    (1, 0): [(0, 512, "s")],
+    (1, 0): [(0, 256, "s"), (256, 512, "s")],
     (0, 1): [(0, 512, "s")],
     (1, 1): [(0, 512, "s")],
 }
-SCALAR_EVAC = {(0, 0), (0, 2), (1, 0), (1, 1), (1, 2), (1, 3)}
+SCALAR_EVAC = {(0, 0), (0, 2), (1, 1), (1, 3)}
 VECTOR_ABS = {(0, 1), (1, 1), (3, 1)}
 
 
@@ -53,7 +53,7 @@ def tile_list_logo_conflict_likeness_kernel(
         idx = lists.tile([P, S // PER_COL], U16, name="idx")
         idx2 = lists.tile([P, S2 // PER_COL], U16, name="idx2")
         tab = [keep.tile([P, T], I32, name="tab%d" % a, align_bytes=64) for a in range(PASSES)]
-        tab_sc = keep.tile([P, T], U8, name="tab_sc", align_bytes=64)
+        tab_sc = keep.tile([P, T], U8, name="tab_sc", tag="tab_sc", align_bytes=64)
         w4 = keep.tile([P, PASSES, 2 * S2], U8, name="w4", align_bytes=64)
         w4_sc = keep.tile([P, PASSES, S2], U8, name="w4_sc", align_bytes=64)
         v_sc = keep.tile([P, S], U8, name="v_sc", align_bytes=64)
@@ -66,6 +66,8 @@ def tile_list_logo_conflict_likeness_kernel(
         warm_in = keep.tile([P, 1], F32, name="warm_in")
         warm_out = keep.tile([P, 1], F32, name="warm_out")
 
+        wq_tag = {(0, 0): "tab_sc"}
+        hq_tag = {(0, 1): "hbf10"}
         w_raw, w_bf, w_q, w_sc, h_bf, h_q, h_sc = {}, {}, {}, {}, {}, {}, {}
         for a in range(PASSES):
             for b in range(PASSES):
@@ -74,10 +76,8 @@ def tile_list_logo_conflict_likeness_kernel(
                     for c0, c1 in LOAD_PIECES[a, b]
                 ]
                 w_bf[a, b] = keep.tile([P, PACK, P, PACK], BF16, name="wbf%d%d" % (a, b), align_bytes=64)
-                w_q[a, b] = keep.tile([P, KP], U32, name="wq%d%d" % (a, b), align_bytes=64)
                 w_sc[a, b] = keep.tile([P, KP], U8, name="wsc%d%d" % (a, b), align_bytes=64)
-                h_bf[a, b] = keep.tile([P, HALF * PACK], BF16, name="hbf%d%d" % (a, b), align_bytes=64)
-                h_q[a, b] = keep.tile([P, HALF], U32, name="hq%d%d" % (a, b), align_bytes=64)
+                h_bf[a, b] = keep.tile([P, HALF * PACK], BF16, name="hbf%d%d" % (a, b), tag="hbf%d%d" % (a, b), align_bytes=64)
                 h_sc[a, b] = keep.tile([P, HALF], U8, name="hsc%d%d" % (a, b), align_bytes=64)
 
         def bank(n):
@@ -89,20 +89,26 @@ def tile_list_logo_conflict_likeness_kernel(
         def load_w(a, b):
             rows = w1[a * KP : (a + 1) * KP, b * KP : (b + 1) * KP].rearrange("(p i) c -> p i c", i=PACK)
             for raw, (c0, c1) in zip(w_raw[a, b], LOAD_PIECES[a, b]):
-                nc.sync.dma_start(raw[:], rows[:, :, c0:c1])
+                if (a, b) == (0, 0):
+                    for i in range(0, PACK, 2):
+                        nc.sync.dma_start(raw[:, i : i + 2, :], rows[:, i : i + 2, c0:c1])
+                else:
+                    nc.sync.dma_start(raw[:], rows[:, :, c0:c1])
 
         def cast_w(a, b):
             for c0, c1, engine in CASTS[a, b]:
                 for raw, (p0, p1) in zip(w_raw[a, b], LOAD_PIECES[a, b]):
                     if p0 <= c0 and c1 <= p1:
-                        src = raw[:, :, c0 - p0 : c1 - p0].rearrange("p i (m t) -> p m i t", t=PACK)
-                        dst = w_bf[a, b][:, :, c0 // PACK : c1 // PACK, :].rearrange("p t m i -> p m i t")
+                        src = raw[:, :, c0 - p0 : c1 - p0].rearrange("p i (m t) -> p m t i", t=PACK)
+                        dst = w_bf[a, b][:, :, c0 // PACK : c1 // PACK, :].rearrange("p t m i -> p m t i")
                         if engine == "s":
                             nc.scalar.copy(dst, src)
                         else:
                             nc.vector.tensor_copy(dst, src)
 
         def quantize_w(a, b):
+            name = "wq%d%d" % (a, b)
+            w_q[a, b] = keep.tile([P, KP], U32, name=name, tag=wq_tag.get((a, b), name), align_bytes=64)
             nc.vector.quantize_mx(
                 out=w_q[a, b][:].bitcast(FP8X4),
                 scales=w_sc[a, b][:],
@@ -141,6 +147,8 @@ def tile_list_logo_conflict_likeness_kernel(
                 nc.vector.tensor_scalar(flat.rearrange("p (j t) -> p j t", t=PACK), src, -1.0, 0.0, ALU.mult, ALU.min)
 
         def quantize_h(b, h):
+            name = "hq%d%d" % (b, h)
+            h_q[b, h] = keep.tile([P, HALF], U32, name=name, tag=hq_tag.get((b, h), name), align_bytes=64)
             nc.vector.quantize_mx(out=h_q[b, h][:].bitcast(FP8X4), scales=h_sc[b, h][:], in_=h_bf[b, h][:])
 
         def skip_product(acc, a, mt, h):
@@ -178,7 +186,8 @@ def tile_list_logo_conflict_likeness_kernel(
             nc.scalar.activation(like[:], gap[:], ACT.Exp, scale=neg_sharp[:, mt : mt + 1])
             nc.sync.dma_start(out[mt * P : (mt + 1) * P, h * HALF : (h + 1) * HALF], like[:])
 
-        nc.vector.memset(tab_sc[:].bitcast(I32), 0)
+        nc.vector.memset(tab_sc[:, 0:2816].bitcast(I32), 0)
+        nc.gpsimd.memset(tab_sc[:, 2816:T].bitcast(I32), 0)
         nc.gpsimd.memset(w4_sc[:].rearrange("p a c -> p (a c)").bitcast(I32), 0)
         nc.gpsimd.memset(v_sc1[:].bitcast(I32), 0)
         nc.vector.memset(warm_in[:], 0.0)
@@ -187,20 +196,20 @@ def tile_list_logo_conflict_likeness_kernel(
         nc.sync.dma_start(idx[:], offs)
         load_w(0, 0)
         nc.sync.dma_start(idx2[:], offs2)
-        load_tab(0)
         for q in range(4):
-            nc.gpsimd.dma_start(
+            nc.sync.dma_start(
                 tab_sc[32 * q : 32 * q + 4 * PASSES, :].bitcast(I32),
                 tab_scales[:, 4 * q : 4 * q + 4, :].bitcast(I32),
             )
+        load_tab(0)
+        load_tab(1)
+        load_w(1, 0)
+        nc.sync.dma_start(w4[:].bitcast(I32), w4_words.rearrange("a p c -> p a c").bitcast(I32))
         for q in range(4):
-            nc.gpsimd.dma_start(
+            nc.sync.dma_start(
                 w4_sc[32 * q : 32 * q + 4, :, :].bitcast(I32),
                 w4_scales[:, 4 * q : 4 * q + 4, :].rearrange("a r c -> r a c").bitcast(I32),
             )
-        load_w(1, 0)
-        load_tab(1)
-        nc.sync.dma_start(w4[:].bitcast(I32), w4_words.rearrange("a p c -> p a c").bitcast(I32))
         load_w(0, 1)
         load_w(1, 1)
         with nc.allow_non_contiguous_dma(reason="one factor for each partition"):
@@ -208,12 +217,12 @@ def tile_list_logo_conflict_likeness_kernel(
         nc.gpsimd.tensor_scalar(neg_sharp[:], sharp_sb[:], -1.0, 0.0, ALU.mult, ALU.add)
 
         nc.vector.tensor_copy(v_sc[:], tab_sc[:].indirect(idx[:]))
-        nc.gpsimd.dma_start(v_sc1[0:100, :].bitcast(I32), v_sc[4:104, :].bitcast(I32))
+        nc.scalar.dma_start(v_sc1[0:100, :].bitcast(I32), v_sc[4:104, :].bitcast(I32))
+        nc.vector.tensor_copy(v2_sc[:], tab_sc[:].indirect(idx2[:]))
         cast_w(0, 0)
         quantize_w(0, 0)
         gather_v(0, 0)
         gather_v(0, 1)
-        nc.vector.tensor_copy(v2_sc[:], tab_sc[:].indirect(idx2[:]))
         gather_v2(0)
 
         tiles = S // JT
@@ -221,10 +230,11 @@ def tile_list_logo_conflict_likeness_kernel(
         for jt in range(tiles):
             first_product(acc[jt], 0, 0, jt)
 
-        cast_w(1, 0)
-        quantize_w(1, 0)
         gather_v(1, 0)
         gather_v(1, 1)
+        cast_w(1, 0)
+        quantize_w(1, 0)
+        gather_v2(1)
 
         for jt in range(tiles):
             first_product(acc[jt], 1, 0, jt)
@@ -242,14 +252,13 @@ def tile_list_logo_conflict_likeness_kernel(
             first_product(acc[jt], 0, 1, jt)
         cast_w(1, 1)
         quantize_w(1, 1)
-        gather_v2(1)
-        quantize_h(0, 1)
         for mt in range(4):
             match_product(res[mt], 0, mt, 0)
         for jt in range(4):
             first_product(acc[jt], 1, 1, jt)
             rectify(acc[jt], 1, jt)
         quantize_h(1, 0)
+        quantize_h(0, 1)
         for jt in range(4, 8):
             acc = bank(jt)
             for a in range(PASSES):

@@ -26,18 +26,18 @@ PER_COL = 16
 
 LOAD_PIECES = {
     (0, 0): [(0, 512)],
-    (1, 0): [(0, 256), (256, 512)],
+    (1, 0): [(0, 512)],
     (0, 1): [(0, 512)],
     (1, 1): [(0, 512)],
 }
 CASTS = {
     (0, 0): [(0, 512, "s")],
-    (1, 0): [(0, 256, "s"), (256, 512, "s")],
+    (1, 0): [(0, 512, "s")],
     (0, 1): [(0, 512, "s")],
     (1, 1): [(0, 512, "s")],
 }
-SCALAR_EVAC = {(0, 0), (0, 2), (1, 1), (1, 3)}
-VECTOR_ABS = {(0, 1), (1, 1), (3, 1)}
+SCALAR_EVAC = {(0, 0), (0, 1), (1, 0), (1, 1), (1, 2), (1, 3), (1, 4), (1, 5)}
+VECTOR_ABS = {(3, 0), (0, 1), (1, 1)}
 
 
 def tile_list_logo_conflict_likeness_kernel(
@@ -48,25 +48,31 @@ def tile_list_logo_conflict_likeness_kernel(
         lists = ctx.enter_context(tc.tile_pool(name="lists", bufs=1))
         keep = ctx.enter_context(tc.tile_pool(name="keep", bufs=1))
         ring = ctx.enter_context(tc.tile_pool(name="ring", bufs=4))
+        reuse = ctx.enter_context(tc.tile_pool(name="reuse", bufs=1))
         psum = ctx.enter_context(tc.psum_pool(name="psum", bufs=1))
 
         idx = lists.tile([P, S // PER_COL], U16, name="idx")
         idx2 = lists.tile([P, S2 // PER_COL], U16, name="idx2")
         tab = [keep.tile([P, T], I32, name="tab%d" % a, align_bytes=64) for a in range(PASSES)]
-        tab_sc = keep.tile([P, T], U8, name="tab_sc", tag="tab_sc", align_bytes=64)
+        tab_sc = reuse.tile([P, T], U8, name="tab_sc", align_bytes=64, offset=0)
         w4 = keep.tile([P, PASSES, 2 * S2], U8, name="w4", align_bytes=64)
         w4_sc = keep.tile([P, PASSES, S2], U8, name="w4_sc", align_bytes=64)
         v_sc = keep.tile([P, S], U8, name="v_sc", align_bytes=64)
         v_sc1 = keep.tile([P, S], U8, name="v_sc1", align_bytes=64)
         v2_sc = keep.tile([P, S2], U8, name="v2_sc", align_bytes=64)
-        v = [[keep.tile([P, HALF], U32, name="v%d_%d" % (a, h), align_bytes=64) for h in range(2)] for a in range(PASSES)]
-        v2 = [keep.tile([P, S2], U32, name="v2_%d" % a, align_bytes=64) for a in range(PASSES)]
+        placed = {"wq00": 0, "v0_0": 2048, "wbf00": 4096, "v0_1": 4096, "v2_0": 6144}
+
+        def own(shape, dtype, name, tag=None):
+            if name in placed:
+                return reuse.tile(shape, dtype, name=name, align_bytes=64, offset=placed[name])
+            return keep.tile(shape, dtype, name=name, tag=tag or name, align_bytes=64)
+
+        v, v2 = {}, {}
         sharp_sb = keep.tile([P, S2 // P], F32, name="sharp_sb")
         neg_sharp = keep.tile([P, S2 // P], F32, name="neg_sharp")
         warm_in = keep.tile([P, 1], F32, name="warm_in")
         warm_out = keep.tile([P, 1], F32, name="warm_out")
 
-        wq_tag = {(0, 0): "tab_sc"}
         hq_tag = {(0, 1): "hbf10"}
         w_raw, w_bf, w_q, w_sc, h_bf, h_q, h_sc = {}, {}, {}, {}, {}, {}, {}
         for a in range(PASSES):
@@ -75,7 +81,7 @@ def tile_list_logo_conflict_likeness_kernel(
                     keep.tile([P, PACK, c1 - c0], F32, name="wraw%d%d_%d" % (a, b, c0))
                     for c0, c1 in LOAD_PIECES[a, b]
                 ]
-                w_bf[a, b] = keep.tile([P, PACK, P, PACK], BF16, name="wbf%d%d" % (a, b), align_bytes=64)
+                w_bf[a, b] = own([P, PACK, P, PACK], BF16, "wbf%d%d" % (a, b))
                 w_sc[a, b] = keep.tile([P, KP], U8, name="wsc%d%d" % (a, b), align_bytes=64)
                 h_bf[a, b] = keep.tile([P, HALF * PACK], BF16, name="hbf%d%d" % (a, b), tag="hbf%d%d" % (a, b), align_bytes=64)
                 h_sc[a, b] = keep.tile([P, HALF], U8, name="hsc%d%d" % (a, b), align_bytes=64)
@@ -107,8 +113,7 @@ def tile_list_logo_conflict_likeness_kernel(
                             nc.vector.tensor_copy(dst, src)
 
         def quantize_w(a, b):
-            name = "wq%d%d" % (a, b)
-            w_q[a, b] = keep.tile([P, KP], U32, name=name, tag=wq_tag.get((a, b), name), align_bytes=64)
+            w_q[a, b] = own([P, KP], U32, "wq%d%d" % (a, b))
             nc.vector.quantize_mx(
                 out=w_q[a, b][:].bitcast(FP8X4),
                 scales=w_sc[a, b][:],
@@ -117,9 +122,11 @@ def tile_list_logo_conflict_likeness_kernel(
 
         def gather_v(a, h):
             cols = slice(h * HALF // PER_COL, (h + 1) * HALF // PER_COL)
-            nc.vector.tensor_copy(v[a][h][:], tab[a][:].bitcast(U32).indirect(idx[:, cols]))
+            v[a, h] = own([P, HALF], U32, "v%d_%d" % (a, h))
+            nc.vector.tensor_copy(v[a, h][:], tab[a][:].bitcast(U32).indirect(idx[:, cols]))
 
         def gather_v2(a):
+            v2[a] = own([P, S2], U32, "v2_%d" % a, "wbf11")
             nc.vector.tensor_copy(v2[a][:], tab[a][:].bitcast(U32).indirect(idx2[:]))
 
         def first_product(acc, a, b, jt):
@@ -129,7 +136,7 @@ def tile_list_logo_conflict_likeness_kernel(
                     out=acc[:, t * JT : (t + 1) * JT],
                     lhsT=w_q[a, b][:, t * P : (t + 1) * P].bitcast(FP8X4),
                     lhsT_scale=w_sc[a, b][:, t * P : (t + 1) * P],
-                    rhs=v[a][h][:, j0 : j0 + JT].bitcast(FP8X4),
+                    rhs=v[a, h][:, j0 : j0 + JT].bitcast(FP8X4),
                     rhs_scale=v_sc[4 * a : P, jt * JT : (jt + 1) * JT],
                     start=(a == 0 and t == 0),
                     stop=(a == PASSES - 1 and t == PACK - 1),
@@ -147,8 +154,7 @@ def tile_list_logo_conflict_likeness_kernel(
                 nc.vector.tensor_scalar(flat.rearrange("p (j t) -> p j t", t=PACK), src, -1.0, 0.0, ALU.mult, ALU.min)
 
         def quantize_h(b, h):
-            name = "hq%d%d" % (b, h)
-            h_q[b, h] = keep.tile([P, HALF], U32, name=name, tag=hq_tag.get((b, h), name), align_bytes=64)
+            h_q[b, h] = own([P, HALF], U32, "hq%d%d" % (b, h), hq_tag.get((b, h)))
             nc.vector.quantize_mx(out=h_q[b, h][:].bitcast(FP8X4), scales=h_sc[b, h][:], in_=h_bf[b, h][:])
 
         def skip_product(acc, a, mt, h):
@@ -157,7 +163,7 @@ def tile_list_logo_conflict_likeness_kernel(
                 out=acc[:],
                 lhsT=w4[:, a, 2 * mt * P : 2 * (mt + 1) * P].bitcast(FP4X4),
                 lhsT_scale=w4_sc[:, a, mt * P : (mt + 1) * P],
-                rhs=v[a][h][:].bitcast(FP8X4),
+                rhs=v[a, h][:].bitcast(FP8X4),
                 rhs_scale=plane[:, h * HALF : (h + 1) * HALF],
                 start=(a == 0),
                 stop=False,
@@ -181,15 +187,18 @@ def tile_list_logo_conflict_likeness_kernel(
                 diff = ring.tile([P, HALF], F32, name="diff")
                 nc.vector.tensor_copy(diff[:], acc[:])
                 nc.vector.scalar_tensor_tensor(gap[:], diff[:], -1.0, diff[:], ALU.mult, ALU.max)
-            else:
-                nc.scalar.activation(gap[:], acc[:], ACT.Abs)
-            nc.scalar.activation(like[:], gap[:], ACT.Exp, scale=neg_sharp[:, mt : mt + 1])
-            nc.sync.dma_start(out[mt * P : (mt + 1) * P, h * HALF : (h + 1) * HALF], like[:])
+            width = HALF // 2 if (mt, h) == (3, 1) else HALF
+            for c0 in range(0, HALF, width):
+                cols = slice(c0, c0 + width)
+                if (mt, h) not in VECTOR_ABS:
+                    nc.scalar.activation(gap[:, cols], acc[:, cols], ACT.Abs)
+                nc.scalar.activation(like[:, cols], gap[:, cols], ACT.Exp, scale=neg_sharp[:, mt : mt + 1])
+                nc.sync.dma_start(out[mt * P : (mt + 1) * P, h * HALF + c0 : h * HALF + c0 + width], like[:, cols])
 
         nc.vector.memset(tab_sc[:, 0:2816].bitcast(I32), 0)
         nc.gpsimd.memset(tab_sc[:, 2816:T].bitcast(I32), 0)
-        nc.gpsimd.memset(w4_sc[:].rearrange("p a c -> p (a c)").bitcast(I32), 0)
-        nc.gpsimd.memset(v_sc1[:].bitcast(I32), 0)
+        nc.vector.memset(w4_sc[:].rearrange("p a c -> p (a c)").bitcast(I32), 0)
+        nc.vector.memset(v_sc1[:].bitcast(I32), 0)
         nc.vector.memset(warm_in[:], 0.0)
         nc.scalar.activation(warm_out[:], warm_in[:], ACT.Exp)
 
@@ -202,15 +211,15 @@ def tile_list_logo_conflict_likeness_kernel(
                 tab_scales[:, 4 * q : 4 * q + 4, :].bitcast(I32),
             )
         load_tab(0)
-        load_tab(1)
         load_w(1, 0)
+        load_tab(1)
         nc.sync.dma_start(w4[:].bitcast(I32), w4_words.rearrange("a p c -> p a c").bitcast(I32))
+        load_w(0, 1)
         for q in range(4):
-            nc.sync.dma_start(
+            nc.gpsimd.dma_start(
                 w4_sc[32 * q : 32 * q + 4, :, :].bitcast(I32),
                 w4_scales[:, 4 * q : 4 * q + 4, :].rearrange("a r c -> r a c").bitcast(I32),
             )
-        load_w(0, 1)
         load_w(1, 1)
         with nc.allow_non_contiguous_dma(reason="one factor for each partition"):
             nc.sync.dma_start(sharp_sb[:], sharp.rearrange("(c p) -> p c", p=P))
@@ -230,11 +239,10 @@ def tile_list_logo_conflict_likeness_kernel(
         for jt in range(tiles):
             first_product(acc[jt], 0, 0, jt)
 
-        gather_v(1, 0)
-        gather_v(1, 1)
         cast_w(1, 0)
         quantize_w(1, 0)
-        gather_v2(1)
+        gather_v(1, 0)
+        gather_v(1, 1)
 
         for jt in range(tiles):
             first_product(acc[jt], 1, 0, jt)
@@ -242,7 +250,6 @@ def tile_list_logo_conflict_likeness_kernel(
 
         cast_w(0, 1)
         quantize_w(0, 1)
-        quantize_h(0, 0)
         res = [bank(mt) for mt in range(4)]
         for a in range(PASSES):
             for mt in range(4):
@@ -252,11 +259,13 @@ def tile_list_logo_conflict_likeness_kernel(
             first_product(acc[jt], 0, 1, jt)
         cast_w(1, 1)
         quantize_w(1, 1)
-        for mt in range(4):
-            match_product(res[mt], 0, mt, 0)
+        quantize_h(0, 0)
+        gather_v2(1)
         for jt in range(4):
             first_product(acc[jt], 1, 1, jt)
             rectify(acc[jt], 1, jt)
+        for mt in range(4):
+            match_product(res[mt], 0, mt, 0)
         quantize_h(1, 0)
         quantize_h(0, 1)
         for jt in range(4, 8):

@@ -32,11 +32,11 @@ LOAD_PIECES = {
 }
 CASTS = {
     (0, 0): [(0, 512, "s")],
-    (1, 0): [(0, 512, "s")],
-    (0, 1): [(0, 512, "s")],
-    (1, 1): [(0, 512, "s")],
+    (1, 0): [(0, 256, "s"), (256, 512, "v")],
+    (0, 1): [(0, 512, "v")],
+    (1, 1): [(0, 512, "v")],
 }
-SCALAR_EVAC = {(0, 0), (0, 1), (1, 0), (1, 1), (1, 2), (1, 3), (1, 4), (1, 5)}
+SCALAR_EVAC = {(0, jt) for jt in range(8)} | {(1, jt) for jt in range(6)}
 VECTOR_ABS = {(3, 0), (0, 1), (1, 1)}
 
 
@@ -47,7 +47,7 @@ def tile_list_logo_conflict_likeness_kernel(
     with ExitStack() as ctx:
         lists = ctx.enter_context(tc.tile_pool(name="lists", bufs=1))
         keep = ctx.enter_context(tc.tile_pool(name="keep", bufs=1))
-        ring = ctx.enter_context(tc.tile_pool(name="ring", bufs=4))
+        ring = ctx.enter_context(tc.tile_pool(name="ring", bufs=8))
         reuse = ctx.enter_context(tc.tile_pool(name="reuse", bufs=1))
         psum = ctx.enter_context(tc.psum_pool(name="psum", bufs=1))
 
@@ -60,7 +60,8 @@ def tile_list_logo_conflict_likeness_kernel(
         v_sc = keep.tile([P, S], U8, name="v_sc", align_bytes=64)
         v_sc1 = keep.tile([P, S], U8, name="v_sc1", align_bytes=64)
         v2_sc = keep.tile([P, S2], U8, name="v2_sc", align_bytes=64)
-        placed = {"wq00": 0, "v0_0": 2048, "wbf00": 4096, "v0_1": 4096, "v2_0": 6144}
+        placed = {"wq00": 0, "v0_0": 2048, "wbf00": 4096, "v0_1": 4096, "v2_0": 6144,
+                  "wraw11_0": 8192, "hbf00": 8192, "hbf01": 12288}
 
         def own(shape, dtype, name, tag=None):
             if name in placed:
@@ -73,17 +74,18 @@ def tile_list_logo_conflict_likeness_kernel(
         warm_in = keep.tile([P, 1], F32, name="warm_in")
         warm_out = keep.tile([P, 1], F32, name="warm_out")
 
-        hq_tag = {(0, 1): "hbf10"}
+        hq_tag = {}
+        pos = {}
         w_raw, w_bf, w_q, w_sc, h_bf, h_q, h_sc = {}, {}, {}, {}, {}, {}, {}
         for a in range(PASSES):
             for b in range(PASSES):
                 w_raw[a, b] = [
-                    keep.tile([P, PACK, c1 - c0], F32, name="wraw%d%d_%d" % (a, b, c0))
+                    own([P, PACK, c1 - c0], F32, "wraw%d%d_%d" % (a, b, c0))
                     for c0, c1 in LOAD_PIECES[a, b]
                 ]
                 w_bf[a, b] = own([P, PACK, P, PACK], BF16, "wbf%d%d" % (a, b))
                 w_sc[a, b] = keep.tile([P, KP], U8, name="wsc%d%d" % (a, b), align_bytes=64)
-                h_bf[a, b] = keep.tile([P, HALF * PACK], BF16, name="hbf%d%d" % (a, b), tag="hbf%d%d" % (a, b), align_bytes=64)
+                pos[a, b] = own([P, HALF * PACK], BF16, "pos%d%d" % (a, b))
                 h_sc[a, b] = keep.tile([P, HALF], U8, name="hsc%d%d" % (a, b), align_bytes=64)
 
         def bank(n):
@@ -145,13 +147,19 @@ def tile_list_logo_conflict_likeness_kernel(
         def rectify(acc, b, jt):
             h, j0 = divmod(jt * JT, HALF)
             src = acc[:].rearrange("p (t j) -> p j t", t=PACK)
-            flat = h_bf[b, h][:, j0 * PACK : (j0 + JT) * PACK]
+            cols = slice(j0 * PACK, (j0 + JT) * PACK)
             if (b, jt) in SCALAR_EVAC:
-                pos = ring.tile([P, JT * PACK], BF16, name="pos")
-                nc.scalar.activation(pos[:].rearrange("p (j t) -> p j t", t=PACK), src, ACT.Relu)
-                nc.vector.tensor_scalar(flat, pos[:], -1.0, None, ALU.mult)
+                nc.scalar.activation(pos[b, h][:, cols].rearrange("p (j t) -> p j t", t=PACK), src, ACT.Relu)
             else:
-                nc.vector.tensor_scalar(flat.rearrange("p (j t) -> p j t", t=PACK), src, -1.0, 0.0, ALU.mult, ALU.min)
+                dst = h_bf[b, h][:, cols].rearrange("p (j t) -> p j t", t=PACK)
+                nc.vector.tensor_scalar(dst, src, -1.0, 0.0, ALU.mult, ALU.min)
+
+        def negate(b, jt0, jt1):
+            h, j0 = divmod(jt0 * JT, HALF)
+            if (b, h) not in h_bf:
+                h_bf[b, h] = own([P, HALF * PACK], BF16, "hbf%d%d" % (b, h))
+            cols = slice(j0 * PACK, (j0 + (jt1 - jt0) * JT) * PACK)
+            nc.vector.tensor_scalar(h_bf[b, h][:, cols], pos[b, h][:, cols], -1.0, None, ALU.mult)
 
         def quantize_h(b, h):
             h_q[b, h] = own([P, HALF], U32, "hq%d%d" % (b, h), hq_tag.get((b, h)))
@@ -259,14 +267,18 @@ def tile_list_logo_conflict_likeness_kernel(
             first_product(acc[jt], 0, 1, jt)
         cast_w(1, 1)
         quantize_w(1, 1)
+        negate(0, 0, 4)
         quantize_h(0, 0)
         gather_v2(1)
         for jt in range(4):
             first_product(acc[jt], 1, 1, jt)
             rectify(acc[jt], 1, jt)
+            if jt % 2 == 1:
+                negate(1, jt - 1, jt + 1)
         for mt in range(4):
             match_product(res[mt], 0, mt, 0)
         quantize_h(1, 0)
+        negate(0, 4, 8)
         quantize_h(0, 1)
         for jt in range(4, 8):
             acc = bank(jt)
@@ -274,10 +286,11 @@ def tile_list_logo_conflict_likeness_kernel(
                 first_product(acc, a, 1, jt)
             rectify(acc, 1, jt)
             if jt == 5:
-                for mt in range(4):
-                    match_product(res[mt], 1, mt, 0)
-                    likeness(res[mt], mt, 0)
+                negate(1, 4, 6)
         quantize_h(1, 1)
+        for mt in range(4):
+            match_product(res[mt], 1, mt, 0)
+            likeness(res[mt], mt, 0)
         for mt in range(4):
             res1 = bank(4 + mt)
             for a in range(PASSES):

from contextlib import ExitStack

import concourse.mybir as mybir

K, T, S, S2 = 1024, 4096, 1024, 512
FLOPS = 2 * K * K * S + 2 * 2 * K * S2 * S

F32 = mybir.dt.float32
BF16 = mybir.dt.bfloat16
I32 = mybir.dt.int32
U32 = mybir.dt.uint32
U16 = mybir.dt.uint16
U8 = mybir.dt.uint8
FP8X4 = mybir.dt.float8_e4m3fn_x4
FP4X4 = mybir.dt.float4_e2m1fn_x4
ALU = mybir.AluOpType
ACT = mybir.ActivationFunctionType

P = 128
PACK = 4
KP = P * PACK
PASSES = K // KP
HALF = 512
JT = 128
PER_COL = 16

LOAD_PIECES = {
    (0, 0): [(0, 512)],
    (1, 0): [(0, 512)],
    (0, 1): [(0, 512)],
    (1, 1): [(0, 512)],
}
CASTS = {
    (0, 0): [(0, 512, "s")],
    (1, 0): [(0, 256, "s"), (256, 512, "v")],
    (0, 1): [(0, 512, "v")],
    (1, 1): [(0, 512, "v")],
}
SCALAR_EVAC = {(0, jt) for jt in range(8)} | {(1, jt) for jt in range(6)}
VECTOR_ABS = {(3, 0), (0, 1), (1, 1)}


def tile_list_logo_conflict_likeness_kernel(
    tc, tab_words, tab_scales, offs, offs2, w1, w4_words, w4_scales, sharp, out
):
    nc = tc.nc
    with ExitStack() as ctx:
        lists = ctx.enter_context(tc.tile_pool(name="lists", bufs=1))
        keep = ctx.enter_context(tc.tile_pool(name="keep", bufs=1))
        ring = ctx.enter_context(tc.tile_pool(name="ring", bufs=8))
        reuse = ctx.enter_context(tc.tile_pool(name="reuse", bufs=1))
        psum = ctx.enter_context(tc.psum_pool(name="psum", bufs=1))

        idx = lists.tile([P, S // PER_COL], U16, name="idx")
        idx2 = lists.tile([P, S2 // PER_COL], U16, name="idx2")
        tab = [keep.tile([P, T], I32, name="tab%d" % a, align_bytes=64) for a in range(PASSES)]
        tab_sc = reuse.tile([P, T], U8, name="tab_sc", align_bytes=64, offset=0)
        w4 = keep.tile([P, PASSES, 2 * S2], U8, name="w4", align_bytes=64)
        w4_sc = keep.tile([P, PASSES, S2], U8, name="w4_sc", align_bytes=64)
        v_sc = keep.tile([P, S], U8, name="v_sc", align_bytes=64)
        v_sc1 = keep.tile([P, S], U8, name="v_sc1", align_bytes=64)
        v2_sc = keep.tile([P, S2], U8, name="v2_sc", align_bytes=64)
        placed = {"wq00": 0, "v0_0": 2048, "wbf00": 4096, "v0_1": 4096, "v2_0": 6144,
                  "wraw11_0": 8192, "hbf00": 8192, "hbf01": 12288}

        def own(shape, dtype, name, tag=None):
            if name in placed:
                return reuse.tile(shape, dtype, name=name, align_bytes=64, offset=placed[name])
            return keep.tile(shape, dtype, name=name, tag=tag or name, align_bytes=64)

        v, v2 = {}, {}
        sharp_sb = keep.tile([P, S2 // P], F32, name="sharp_sb")
        neg_sharp = keep.tile([P, S2 // P], F32, name="neg_sharp")
        warm_in = keep.tile([P, 1], F32, name="warm_in")
        warm_out = keep.tile([P, 1], F32, name="warm_out")

        hq_tag = {}
        pos = {}
        w_raw, w_bf, w_q, w_sc, h_bf, h_q, h_sc = {}, {}, {}, {}, {}, {}, {}
        for a in range(PASSES):
            for b in range(PASSES):
                w_raw[a, b] = [
                    own([P, PACK, c1 - c0], F32, "wraw%d%d_%d" % (a, b, c0))
                    for c0, c1 in LOAD_PIECES[a, b]
                ]
                w_bf[a, b] = own([P, PACK, P, PACK], BF16, "wbf%d%d" % (a, b))
                w_sc[a, b] = keep.tile([P, KP], U8, name="wsc%d%d" % (a, b), align_bytes=64)
                pos[a, b] = own([P, HALF * PACK], BF16, "pos%d%d" % (a, b))
                h_sc[a, b] = keep.tile([P, HALF], U8, name="hsc%d%d" % (a, b), align_bytes=64)

        def bank(n):
            return psum.tile([P, HALF], F32, name="bank%d" % n, tag="bank%d" % n)

        def load_tab(a):
            nc.sync.dma_start(tab[a][:], tab_words[a].rearrange("p n i -> p (n i)").bitcast(I32))

        def load_w(a, b):
            rows = w1[a * KP : (a + 1) * KP, b * KP : (b + 1) * KP].rearrange("(p i) c -> p i c", i=PACK)
            for raw, (c0, c1) in zip(w_raw[a, b], LOAD_PIECES[a, b]):
                if (a, b) == (0, 0):
                    for i in range(0, PACK, 2):
                        nc.sync.dma_start(raw[:, i : i + 2, :], rows[:, i : i + 2, c0:c1])
                else:
                    nc.sync.dma_start(raw[:], rows[:, :, c0:c1])

        def cast_w(a, b):
            for c0, c1, engine in CASTS[a, b]:
                for raw, (p0, p1) in zip(w_raw[a, b], LOAD_PIECES[a, b]):
                    if p0 <= c0 and c1 <= p1:
                        src = raw[:, :, c0 - p0 : c1 - p0].rearrange("p i (m t) -> p m t i", t=PACK)
                        dst = w_bf[a, b][:, :, c0 // PACK : c1 // PACK, :].rearrange("p t m i -> p m t i")
                        if engine == "s":
                            nc.scalar.copy(dst, src)
                        else:
                            nc.vector.tensor_copy(dst, src)

        def quantize_w(a, b):
            w_q[a, b] = own([P, KP], U32, "wq%d%d" % (a, b))
            nc.vector.quantize_mx(
                out=w_q[a, b][:].bitcast(FP8X4),
                scales=w_sc[a, b][:],
                in_=w_bf[a, b][:].rearrange("p t m i -> p (t m i)"),
            )

        def gather_v(a, h):
            cols = slice(h * HALF // PER_COL, (h + 1) * HALF // PER_COL)
            v[a, h] = own([P, HALF], U32, "v%d_%d" % (a, h))
            nc.vector.tensor_copy(v[a, h][:], tab[a][:].bitcast(U32).indirect(idx[:, cols]))

        def gather_v2(a):
            v2[a] = own([P, S2], U32, "v2_%d" % a, "wbf11")
            nc.vector.tensor_copy(v2[a][:], tab[a][:].bitcast(U32).indirect(idx2[:]))

        def first_product(acc, a, b, jt):
            h, j0 = divmod(jt * JT, HALF)
            for t in range(PACK):
                nc.tensor.matmul_mx(
                    out=acc[:, t * JT : (t + 1) * JT],
                    lhsT=w_q[a, b][:, t * P : (t + 1) * P].bitcast(FP8X4),
                    lhsT_scale=w_sc[a, b][:, t * P : (t + 1) * P],
                    rhs=v[a, h][:, j0 : j0 + JT].bitcast(FP8X4),
                    rhs_scale=v_sc[4 * a : P, jt * JT : (jt + 1) * JT],
                    start=(a == 0 and t == 0),
                    stop=(a == PASSES - 1 and t == PACK - 1),
                )

        def rectify(acc, b, jt):
            h, j0 = divmod(jt * JT, HALF)
            src = acc[:].rearrange("p (t j) -> p j t", t=PACK)
            cols = slice(j0 * PACK, (j0 + JT) * PACK)
            if (b, jt) in SCALAR_EVAC:
                nc.scalar.activation(pos[b, h][:, cols].rearrange("p (j t) -> p j t", t=PACK), src, ACT.Relu)
            else:
                dst = h_bf[b, h][:, cols].rearrange("p (j t) -> p j t", t=PACK)
                nc.vector.tensor_scalar(dst, src, -1.0, 0.0, ALU.mult, ALU.min)

        def negate(b, jt0, jt1):
            h, j0 = divmod(jt0 * JT, HALF)
            if (b, h) not in h_bf:
                h_bf[b, h] = own([P, HALF * PACK], BF16, "hbf%d%d" % (b, h))
            cols = slice(j0 * PACK, (j0 + (jt1 - jt0) * JT) * PACK)
            nc.vector.tensor_scalar(h_bf[b, h][:, cols], pos[b, h][:, cols], -1.0, None, ALU.mult)

        def quantize_h(b, h):
            h_q[b, h] = own([P, HALF], U32, "hq%d%d" % (b, h), hq_tag.get((b, h)))
            nc.vector.quantize_mx(out=h_q[b, h][:].bitcast(FP8X4), scales=h_sc[b, h][:], in_=h_bf[b, h][:])

        def skip_product(acc, a, mt, h):
            plane = v_sc if a == 0 else v_sc1
            nc.tensor.matmul_mx(
                out=acc[:],
                lhsT=w4[:, a, 2 * mt * P : 2 * (mt + 1) * P].bitcast(FP4X4),
                lhsT_scale=w4_sc[:, a, mt * P : (mt + 1) * P],
                rhs=v[a, h][:].bitcast(FP8X4),
                rhs_scale=plane[:, h * HALF : (h + 1) * HALF],
                start=(a == 0),
                stop=False,
            )

        def match_product(acc, b, mt, h):
            nc.tensor.matmul_mx(
                out=acc[:],
                lhsT=v2[b][:, mt * P : (mt + 1) * P].bitcast(FP8X4),
                lhsT_scale=v2_sc[4 * b : P, mt * P : (mt + 1) * P],
                rhs=h_q[b, h][:].bitcast(FP8X4),
                rhs_scale=h_sc[b, h][:],
                start=False,
                stop=(b == PASSES - 1),
            )

        def likeness(acc, mt, h):
            gap = ring.tile([P, HALF], F32, name="gap")
            like = ring.tile([P, HALF], F32, name="like")
            if (mt, h) in VECTOR_ABS:
                diff = ring.tile([P, HALF], F32, name="diff")
                nc.vector.tensor_copy(diff[:], acc[:])
                nc.vector.scalar_tensor_tensor(gap[:], diff[:], -1.0, diff[:], ALU.mult, ALU.max)
            width = HALF // 2 if (mt, h) == (3, 1) else HALF
            for c0 in range(0, HALF, width):
                cols = slice(c0, c0 + width)
                if (mt, h) not in VECTOR_ABS:
                    nc.scalar.activation(gap[:, cols], acc[:, cols], ACT.Abs)
                nc.scalar.activation(like[:, cols], gap[:, cols], ACT.Exp, scale=neg_sharp[:, mt : mt + 1])
                nc.sync.dma_start(out[mt * P : (mt + 1) * P, h * HALF + c0 : h * HALF + c0 + width], like[:, cols])

        nc.vector.memset(tab_sc[:, 0:2816].bitcast(I32), 0)
        nc.gpsimd.memset(tab_sc[:, 2816:T].bitcast(I32), 0)
        nc.vector.memset(w4_sc[:].rearrange("p a c -> p (a c)").bitcast(I32), 0)
        nc.vector.memset(v_sc1[:].bitcast(I32), 0)
        nc.vector.memset(warm_in[:], 0.0)
        nc.scalar.activation(warm_out[:], warm_in[:], ACT.Exp)

        nc.sync.dma_start(idx[:], offs)
        load_w(0, 0)
        nc.sync.dma_start(idx2[:], offs2)
        for q in range(4):
            nc.sync.dma_start(
                tab_sc[32 * q : 32 * q + 4 * PASSES, :].bitcast(I32),
                tab_scales[:, 4 * q : 4 * q + 4, :].bitcast(I32),
            )
        load_tab(0)
        load_w(1, 0)
        load_tab(1)
        nc.sync.dma_start(w4[:].bitcast(I32), w4_words.rearrange("a p c -> p a c").bitcast(I32))
        load_w(0, 1)
        for q in range(4):
            nc.gpsimd.dma_start(
                w4_sc[32 * q : 32 * q + 4, :, :].bitcast(I32),
                w4_scales[:, 4 * q : 4 * q + 4, :].rearrange("a r c -> r a c").bitcast(I32),
            )
        load_w(1, 1)
        with nc.allow_non_contiguous_dma(reason="one factor for each partition"):
            nc.sync.dma_start(sharp_sb[:], sharp.rearrange("(c p) -> p c", p=P))
        nc.gpsimd.tensor_scalar(neg_sharp[:], sharp_sb[:], -1.0, 0.0, ALU.mult, ALU.add)

        nc.vector.tensor_copy(v_sc[:], tab_sc[:].indirect(idx[:]))
        nc.scalar.dma_start(v_sc1[0:100, :].bitcast(I32), v_sc[4:104, :].bitcast(I32))
        nc.vector.tensor_copy(v2_sc[:], tab_sc[:].indirect(idx2[:]))
        cast_w(0, 0)
        quantize_w(0, 0)
        gather_v(0, 0)
        gather_v(0, 1)
        gather_v2(0)

        tiles = S // JT
        acc = [bank(n) for n in range(tiles)]
        for jt in range(tiles):
            first_product(acc[jt], 0, 0, jt)

        cast_w(1, 0)
        quantize_w(1, 0)
        gather_v(1, 0)
        gather_v(1, 1)

        for jt in range(tiles):
            first_product(acc[jt], 1, 0, jt)
            rectify(acc[jt], 0, jt)

        cast_w(0, 1)
        quantize_w(0, 1)
        res = [bank(mt) for mt in range(4)]
        for a in range(PASSES):
            for mt in range(4):
                skip_product(res[mt], a, mt, 0)
        acc = [bank(4 + n) for n in range(4)]
        for jt in range(4):
            first_product(acc[jt], 0, 1, jt)
        cast_w(1, 1)
        quantize_w(1, 1)
        negate(0, 0, 4)
        quantize_h(0, 0)
        gather_v2(1)
        for jt in range(4):
            first_product(acc[jt], 1, 1, jt)
            rectify(acc[jt], 1, jt)
            if jt % 2 == 1:
                negate(1, jt - 1, jt + 1)
        for mt in range(4):
            match_product(res[mt], 0, mt, 0)
        quantize_h(1, 0)
        negate(0, 4, 8)
        quantize_h(0, 1)
        for jt in range(4, 8):
            acc = bank(jt)
            for a in range(PASSES):
                first_product(acc, a, 1, jt)
            rectify(acc, 1, jt)
            if jt == 5:
                negate(1, 4, 6)
        quantize_h(1, 1)
        for mt in range(4):
            match_product(res[mt], 1, mt, 0)
            likeness(res[mt], mt, 0)
        for mt in range(4):
            res1 = bank(4 + mt)
            for a in range(PASSES):
                skip_product(res1, a, mt, 1)
            for b in range(PASSES):
                match_product(res1, b, mt, 1)
            likeness(res1, mt, 1)
